import numpy as np
import ml_dtypes


def mxq(x, axis, fmt="e4m3"):
    dtype, down = {"e4m3": (ml_dtypes.float8_e4m3fn, 7), "e5m2": (ml_dtypes.float8_e5m2, 14)}[fmt]
    v = np.moveaxis(np.asarray(x, np.float32).astype(ml_dtypes.bfloat16).astype(np.float64), axis, -1)
    blocks = v.reshape(v.shape[:-1] + (-1, 32))
    amax = np.abs(blocks).max(-1, keepdims=True)
    byte = np.maximum(np.where(amax > 0, np.frexp(amax)[1] - 1 + 127, 0) - down, 1)
    scale = np.exp2(byte - 127.0)
    codes = (blocks / scale).astype(np.float32).astype(dtype).astype(np.float64)
    return np.moveaxis((codes * scale).reshape(v.shape), -1, axis)


WIDE = False


def mx_kscale(k):
    if not WIDE:
        return np.ones(k)
    levels = np.array([10, -10, 5, -5, 0])
    if k % 512:
        return np.exp2(np.random.permutation(np.resize(levels, k // 32))).repeat(32)
    a = np.empty((k // 512, 16))
    for p in range(k // 512):
        a[p, :8] = np.random.permutation(np.resize(levels, 8))
        for g in range(8):
            far = levels[np.abs(levels - a[p, g]) >= 10]
            a[p, g + 8] = far[np.random.randint(len(far))]
    return np.exp2(a.ravel()).repeat(32)


def f64(x):
    return np.asarray(x).astype(np.float64)


def striped(idx):
    return np.tile(idx.reshape(-1, 16).T, (8, 1)).astype(np.uint16)


def unstriped(offs):
    return offs[:16].T.reshape(-1).astype(np.int64)


def striped8(idx):
    return np.concatenate([x.reshape(-1, 16).T for x in idx]).astype(np.uint16)


def runs(offs, k):
    lists = np.stack([offs[16 * r : 16 * r + 16].T.reshape(-1) for r in range(8)]).astype(np.int64)
    return lists[np.arange(k) % 512 // 64]


def pack_weight(w):
    k, n = w.shape
    w = f64(np.asarray(w, np.float32).astype(ml_dtypes.bfloat16)).reshape(k // 32, 32, n)
    amax = np.abs(w).max(1)
    byte = np.clip(np.where(amax > 0, np.frexp(amax)[1] - 1 + 127 - 7, 1), 1, 254)
    scaled = (w * np.exp2(127.0 - byte)[:, None, :]).reshape(k, n).astype(np.float32)
    words = np.ascontiguousarray(scaled.reshape(k // 512, 128, 4, n).transpose(0, 1, 3, 2)).astype(ml_dtypes.float8_e4m3fn).view(np.uint8)
    return words, np.ascontiguousarray(byte.astype(np.uint8).reshape(k // 512, 16, n))


def unpack_weight(words, scales):
    g, p, n, _ = words.shape
    vals = np.ascontiguousarray(words).view(ml_dtypes.float8_e4m3fn).astype(np.float64) * np.repeat(np.exp2(scales.astype(np.float64) - 127.0), 8, axis=1)[..., None]
    return vals.transpose(0, 1, 3, 2).reshape(g * 512, n)


def sigmoid(v):
    return 1.0 / (1.0 + np.exp(-np.maximum(v, -700.0)))


K, T, S, H, C, G = 512, 1024, 512, 512, 512, 2048


def setup_inputs():
    n = np.random.standard_normal
    s = mx_kscale(K)[:, None]
    packed_xT = pack_weight(n((K, T)) * s)
    packed_dT = pack_weight(n((K, G)) / s)
    return {
        "x_words": packed_xT[0],
        "x_scales": packed_xT[1],
        "w1": (n((K, H)) / np.sqrt(K) / s).astype(np.float32),
        "gs": (np.random.uniform(0.5, 1.5, (K, 1)) / s).astype(np.float32),
        "gk": (np.random.uniform(0.5, 1.5, (K, 1)) * s).astype(np.float32),
        "d_words": packed_dT[0],
        "d_scales": packed_dT[1],
        "offs": striped(np.random.permutation(T)[:S]),
        "n1": striped8(np.stack([np.random.permutation(S) for _ in range(8)])),
        "n2": striped8(np.stack([np.random.permutation(S) for _ in range(8)])),
        "n3": striped8(np.stack([np.random.permutation(S) for _ in range(8)])),
        "n4": striped8(np.stack([np.random.permutation(S) for _ in range(8)])),
        "cand": striped(np.random.permutation(T)[:C]),
        "k1": striped8(np.random.randint(0, G, (8, H))),
        "n5": striped(np.random.permutation(S)),
        "n6": striped(np.random.permutation(S)),
    }


def reference(x_words, x_scales, w1, gs, gk, d_words, d_scales, offs, n1, n2, n3, n4, cand, k1, n5, n6):
    x_cand = unpack_weight(x_words, x_scales)[:, unstriped(cand)]
    xq = unpack_weight(x_words, x_scales)[:, unstriped(offs)]
    y = mxq(f64(w1), 0, "e4m3").T @ xq
    st = y[np.arange(H)[:, None], runs(n1, H)] - y
    z = f64(gs) * (y * (sigmoid(st[np.arange(H)[:, None], runs(n2, H)])))
    a = 0.0625 * ((x_cand.T @ mxq(z, 0, "e4m3")))
    d_k1 = unpack_weight(d_words, d_scales)[np.arange(K)[:, None], runs(k1, K)]
    sq = (y) ** 2
    z2 = f64(gk) * ((y[np.arange(H)[:, None], runs(n4, H)]) / (np.sqrt(sq + sq[np.arange(H)[:, None], runs(n3, H)] + 0.25)))
    b = 0.0625 * ((d_k1.T @ mxq(z2, 0, "e4m3")))
    return a + (sigmoid(b[:, unstriped(n6)] - b)) * (a[:, unstriped(n5)] - a)

@@ -1,0 +1,238 @@
+from contextlib import ExitStack
+
+import concourse.mybir as mybir
+
+K, T, S, H, C, G = 512, 1024, 512, 512, 512, 2048
+FLOPS = 2 * K * H * S + 2 * K * C * S + 2 * K * H * S
+
+F32 = mybir.dt.float32
+BF16 = mybir.dt.bfloat16
+I32 = mybir.dt.int32
+U32 = mybir.dt.uint32
+U16 = mybir.dt.uint16
+U8 = mybir.dt.uint8
+FP8X4 = mybir.dt.float8_e4m3fn_x4
+ACT = mybir.ActivationFunctionType
+ALU = mybir.AluOpType
+
+P = 128
+PACK = 4
+WINDOW = 2 * S
+SCORE_SCALE = 0.0625
+
+
+def tile_picked_cdkeypullbhopdrms_none_p_kernel(
+    tc, x_words, x_scales, w1, gs, gk, d_words, d_scales, offs, n1, n2, n3, n4, cand, k1, n5, n6, out
+):
+    nc = tc.nc
+    with ExitStack() as ctx:
+        lists = ctx.enter_context(tc.tile_pool(name="lists", bufs=1))
+        keep = ctx.enter_context(tc.tile_pool(name="keep", bufs=1))
+        head = ctx.enter_context(tc.tile_pool(name="head", bufs=1))
+        psum = ctx.enter_context(tc.psum_pool(name="psum", bufs=1))
+
+        def load_list(src, name):
+            tile = lists.tile([P, S // 16], U16, name=name)
+            nc.sync.dma_start(tile[:], src)
+            return tile
+
+        def sb(shape, dtype, name, tag=None):
+            return keep.tile(shape, dtype, name=name, tag=tag or name, align_bytes=64)
+
+        x_w = sb([P, T], U32, "x_w")
+        x_s = sb([P, T], U8, "x_s")
+        d_w = sb([P, G], U32, "d_w")
+        d_s = sb([P, G], U8, "d_s")
+        nc.gpsimd.memset(x_s[:].bitcast(I32), 0)
+        nc.vector.memset(d_s[:].bitcast(I32), 0)
+        quarter = sb([P, 1], F32, "quarter")
+        nc.vector.memset(quarter[:], 0.25)
+
+        offs_t = load_list(offs, "offs_t")
+        cand_t = load_list(cand, "cand_t")
+        w_rows = w1.rearrange("(p j) c -> p j c", j=PACK)
+        w_raw = [sb([P, PACK, H // 2], F32, f"w_raw{h}") for h in range(2)]
+        nc.sync.dma_start(w_raw[0][:], w_rows[:, :, : H // 2])
+        xs_rows = x_scales[0].rearrange("(q r) c -> r q c", r=4)
+        for r in range(4):
+            nc.sync.dma_start(x_s[r:P:32, :].bitcast(I32), xs_rows[r].bitcast(I32))
+        nc.sync.dma_start(w_raw[1][:], w_rows[:, :, H // 2 :])
+        nc.sync.dma_start(x_w[:].bitcast(I32), x_words[0].rearrange("p n t -> p (n t)").bitcast(I32))
+        k1_t = load_list(k1, "k1_t")
+        ds_rows = d_scales[0].rearrange("(r e) c -> e r c", e=2)
+        for e in range(2):
+            nc.sync.dma_start(d_s[e:P:16, :].bitcast(I32), ds_rows[e].bitcast(I32))
+        nc.sync.dma_start(d_w[:].bitcast(I32), d_words[0].rearrange("p n t -> p (n t)").bitcast(I32))
+        n3_t = load_list(n3, "n3_t")
+        n4_t = load_list(n4, "n4_t")
+        n1_t = load_list(n1, "n1_t")
+        n2_t = load_list(n2, "n2_t")
+        gs_t = sb([P, PACK], F32, "gs_t")
+        gk_t = sb([P, PACK], F32, "gk_t")
+        nc.sync.dma_start(gk_t[:], gk.rearrange("(p t) o -> p (t o)", t=PACK))
+        nc.sync.dma_start(gs_t[:], gs.rearrange("(p t) o -> p (t o)", t=PACK))
+        n6_t = load_list(n6, "n6_t")
+        n5_t = load_list(n5, "n5_t")
+
+        def pick(table, offsets, dtype, name, offset=None):
+            if offset is None:
+                picked = sb([P, S], dtype, name)
+            else:
+                picked = head.tile([P, S], dtype, name=name, align_bytes=64, offset=offset)
+            nc.vector.tensor_copy(picked[:], table[:].indirect(offsets[:]))
+            return picked
+
+        xq_s = pick(x_s, offs_t, U8, "xq_s")
+        xc_s = pick(x_s, cand_t, U8, "xc_s")
+        xq_w = pick(x_w, offs_t, U32, "xq_w")
+
+        w_bf = head.tile([P, PACK * H], BF16, name="w_bf", align_bytes=64, offset=0)
+        w_view = w_bf[:].rearrange("p (t m j) -> p m j t", t=PACK, j=PACK)
+        for h in range(2):
+            nc.scalar.copy(
+                out=w_view[:, h * 64 : (h + 1) * 64, :, :],
+                in_=w_raw[h][:].rearrange("p j (m t) -> p m j t", t=PACK),
+            )
+
+        def quantize(src, name):
+            codes = sb([P, S], U32, name + "_w")
+            scales = sb([P, S], U8, name + "_s")
+            nc.vector.quantize_mx(out=codes[:].bitcast(FP8X4), scales=scales[:], in_=src[:])
+            return codes, scales
+
+        w_w, w_s = quantize(w_bf, "wq")
+        xc_w = pick(x_w, cand_t, U32, "xc_w", 512)
+        dk_g = pick(d_s, k1_t, U8, "dk_g", 0)
+        dk_w = pick(d_w, k1_t, U32, "dk_w", 2560)
+        dk_s = sb([P, H], U8, "dk_s")
+        nc.vector.tensor_copy(dk_s[:].bitcast(I32), dk_g[:].bitcast(I32))
+        for e in range(2):
+            nc.gpsimd.dma_start(dk_s[2 + e : P : 32, :].bitcast(I32), dk_g[16 + e : P : 32, :].bitcast(I32))
+
+        def product(lhs_w, lhs_s, rhs_w, rhs_s, block, bank):
+            acc = psum.tile([P, S], F32, name=f"acc{bank}", tag=f"bank{bank}")
+            cols = slice(block * P, (block + 1) * P)
+            nc.tensor.matmul_mx(
+                out=acc[:],
+                lhsT=lhs_w[:, cols].bitcast(FP8X4),
+                lhsT_scale=lhs_s[:, cols],
+                rhs=rhs_w[:].bitcast(FP8X4),
+                rhs_scale=rhs_s[:],
+                start=True,
+                stop=True,
+            )
+            return acc
+
+        y_win, y_pl, sq_win, sq_pl = [], [], [], []
+        y_acc = [product(w_w, w_s, xq_w, xq_s, t, t) for t in range(PACK)]
+        for t in range(PACK):
+            acc = y_acc[t]
+            sq_w = sb([P, WINDOW], F32, f"sq_win{t}")
+            nc.scalar.activation(sq_w[:, :S], acc[:], ACT.Square)
+            sq_p = sb([P, S], F32, f"sq_pl{t}")
+            nc.sync.dma_start(sq_p[:], sq_w[:, :S])
+            sq_win.append(sq_w)
+            sq_pl.append(sq_p)
+        for t in range(PACK):
+            y_w = sb([P, WINDOW], F32, f"y_win{t}")
+            nc.scalar.copy(out=y_w[:, :S], in_=y_acc[t][:])
+            y_p = sb([P, S], F32, f"y_pl{t}")
+            nc.sync.dma_start(y_p[:], y_w[:, :S])
+            y_win.append(y_w)
+            y_pl.append(y_p)
+
+        y4, st = [], []
+        for t in range(PACK):
+            g = sb([P, S], F32, f"y4_{t}")
+            nc.scalar.activation(g[:], y_win[t][:].indirect(n4_t[:]), ACT.Copy)
+            y4.append(g)
+        den = sb([P, PACK * S], F32, "den", "den")
+        for t in range(PACK):
+            nc.vector.tensor_tensor(
+                den[:, t * S : (t + 1) * S], sq_win[t][:].indirect(n3_t[:]), sq_pl[t][:], ALU.add
+            )
+        rs = sb([P, PACK * S], F32, "rs")
+        nc.scalar.activation(rs[:], den[:], ACT.Abs_reciprocal_sqrt, bias=quarter[:])
+        for t in range(PACK):
+            s = sb([P, WINDOW], F32, f"st{t}", f"sq_win{PACK - 1 - t}")
+            nc.vector.tensor_tensor(s[:, :S], y_win[t][:].indirect(n1_t[:]), y_pl[t][:], ALU.subtract)
+            st.append(s)
+
+        def interleave(planes, name):
+            woven = sb([P, S, PACK], BF16, name)
+            nc.vector.tensor_copy(
+                out=woven[:].rearrange("p (c i) t -> p c t i", i=4),
+                in_=planes[:].rearrange("p t (c i) -> p c t i", i=4),
+            )
+            return woven
+
+        z2_pl = sb([P, PACK, S], BF16, "z2_pl")
+        for t in range(PACK):
+            nc.vector.scalar_tensor_tensor(
+                z2_pl[:, t, :], y4[t][:], gk_t[:, t : t + 1], rs[:, t * S : (t + 1) * S], ALU.mult, ALU.mult
+            )
+        sig = sb([P, PACK * S], F32, "sig", "den")
+        for t in range(PACK):
+            nc.scalar.activation(sig[:, t * S : (t + 1) * S], st[t][:].indirect(n2_t[:]), ACT.Sigmoid)
+        z2_bf = interleave(z2_pl, "z2_bf")
+        z_pl = sb([P, PACK, S], BF16, "z_pl", "z2_pl")
+
+        def z_plane(t):
+            nc.vector.scalar_tensor_tensor(
+                z_pl[:, t, :], y_pl[t][:], gs_t[:, t : t + 1], sig[:, t * S : (t + 1) * S], ALU.mult, ALU.mult
+            )
+
+        z_plane(0)
+        z2_w = sb([P, S], U32, "z2_w")
+        z2_s = sb([P, S], U8, "z2_s")
+        nc.vector.quantize_mx(
+            out=z2_w[:].bitcast(FP8X4), scales=z2_s[:], in_=z2_bf[:].rearrange("p c t -> p (c t)")
+        )
+        for t in range(1, PACK):
+            z_plane(t)
+        z_bf = interleave(z_pl, "z_bf")
+        z_w = sb([P, S], U32, "z_w")
+        z_s = sb([P, S], U8, "z_s")
+        nc.vector.quantize_mx(
+            out=z_w[:].bitcast(FP8X4), scales=z_s[:], in_=z_bf[:].rearrange("p c t -> p (c t)")
+        )
+
+        b_win, b6, a_win, gate = {}, {}, {}, {}
+
+        def keys(m, bank):
+            acc = product(dk_w, dk_s, z2_w, z2_s, m, bank)
+            b_win[m] = sb([P, WINDOW], F32, f"b_win{m}")
+            nc.scalar.activation(b_win[m][:, :S], acc[:], ACT.Copy, scale=SCORE_SCALE)
+            b6[m] = sb([P, S], F32, f"b6_{m}")
+            nc.scalar.activation(b6[m][:], b_win[m][:].indirect(n6_t[:]), ACT.Copy)
+
+        def candidates(m, bank):
+            acc = product(xc_w, xc_s, z_w, z_s, m, bank)
+            diff = sb([P, S], F32, f"diff{m}")
+            nc.vector.tensor_tensor(diff[:], b6[m][:], b_win[m][:, :S], ALU.subtract)
+            a_win[m] = sb([P, WINDOW], F32, f"a_win{m}")
+            nc.scalar.activation(a_win[m][:, :S], acc[:], ACT.Copy, scale=SCORE_SCALE)
+            gate[m] = sb([P, S], F32, f"gate{m}")
+            nc.scalar.activation(gate[m][:], diff[:], ACT.Sigmoid)
+
+        def blend(m):
+            rest = sb([P, S], F32, f"rest{m}")
+            nc.vector.scalar_tensor_tensor(rest[:], gate[m][:], 1.0, a_win[m][:, :S], ALU.subtract, ALU.mult)
+            pull = sb([P, S], F32, f"pull{m}")
+            nc.vector.tensor_tensor(pull[:], a_win[m][:].indirect(n5_t[:]), gate[m][:], ALU.mult)
+            res = sb([P, S], F32, f"res{m}")
+            nc.vector.tensor_tensor(res[:], pull[:], rest[:], ALU.subtract)
+            nc.sync.dma_start(out[m * P : (m + 1) * P, :], res[:])
+
+        keys(0, 4)
+        keys(1, 5)
+        candidates(0, 6)
+        candidates(1, 7)
+        keys(2, 6)
+        keys(3, 7)
+        blend(0)
+        blend(1)
+        candidates(2, 4)
+        candidates(3, 5)
+        blend(2)
+        blend(3)

@@ -29,7 +29,11 @@ def tile_picked_cdkeypullbhopdrms_none_p_kernel(
         lists = ctx.enter_context(tc.tile_pool(name="lists", bufs=1))
         keep = ctx.enter_context(tc.tile_pool(name="keep", bufs=1))
         head = ctx.enter_context(tc.tile_pool(name="head", bufs=1))
+        mid = ctx.enter_context(tc.tile_pool(name="mid", bufs=1))
         psum = ctx.enter_context(tc.psum_pool(name="psum", bufs=1))
+
+        def placed(shape, dtype, name, kib):
+            return mid.tile(shape, dtype, name=name, align_bytes=64, offset=kib * 1024)
 
         def load_list(src, name):
             tile = lists.tile([P, S // 16], U16, name=name)
@@ -43,21 +47,26 @@ def tile_picked_cdkeypullbhopdrms_none_p_kernel(
         x_s = sb([P, T], U8, "x_s")
         d_w = sb([P, G], U32, "d_w")
         d_s = sb([P, G], U8, "d_s")
-        nc.gpsimd.memset(x_s[:].bitcast(I32), 0)
-        nc.vector.memset(d_s[:].bitcast(I32), 0)
+        nc.gpsimd.memset(d_s[:].bitcast(I32), 0)
         quarter = sb([P, 1], F32, "quarter")
-        nc.vector.memset(quarter[:], 0.25)
+        sixteen = sb([P, 1], F32, "sixteen")
+        nc.vector.memset(sixteen[:], 16.0)
+        nc.scalar.activation(quarter[:], sixteen[:], ACT.Abs_reciprocal_sqrt)
 
         offs_t = load_list(offs, "offs_t")
+        for q in range(4):
+            rows = x_scales[0, 4 * q : 4 * q + 4, :].bitcast(I32)
+            nc.sync.dma_start(
+                x_s[32 * q : 32 * (q + 1), :].bitcast(I32), rows.unsqueeze(0).to_broadcast([8, 4, T // 4])
+            )
         cand_t = load_list(cand, "cand_t")
         w_rows = w1.rearrange("(p j) c -> p j c", j=PACK)
-        w_raw = [sb([P, PACK, H // 2], F32, f"w_raw{h}") for h in range(2)]
-        nc.sync.dma_start(w_raw[0][:], w_rows[:, :, : H // 2])
-        xs_rows = x_scales[0].rearrange("(q r) c -> r q c", r=4)
-        for r in range(4):
-            nc.sync.dma_start(x_s[r:P:32, :].bitcast(I32), xs_rows[r].bitcast(I32))
-        nc.sync.dma_start(w_raw[1][:], w_rows[:, :, H // 2 :])
+        w_cuts = [0, H // 2, 3 * H // 4, H]
+        w_raw = [sb([P, PACK, w_cuts[h + 1] - w_cuts[h]], F32, f"w_raw{h}") for h in range(3)]
+        nc.sync.dma_start(w_raw[0][:], w_rows[:, :, : w_cuts[1]])
         nc.sync.dma_start(x_w[:].bitcast(I32), x_words[0].rearrange("p n t -> p (n t)").bitcast(I32))
+        for h in (1, 2):
+            nc.sync.dma_start(w_raw[h][:], w_rows[:, :, w_cuts[h] : w_cuts[h + 1]])
         k1_t = load_list(k1, "k1_t")
         ds_rows = d_scales[0].rearrange("(r e) c -> e r c", e=2)
         for e in range(2):
@@ -88,26 +97,28 @@ def tile_picked_cdkeypullbhopdrms_none_p_kernel(
 
         w_bf = head.tile([P, PACK * H], BF16, name="w_bf", align_bytes=64, offset=0)
         w_view = w_bf[:].rearrange("p (t m j) -> p m j t", t=PACK, j=PACK)
-        for h in range(2):
+        for h in range(3):
             nc.scalar.copy(
-                out=w_view[:, h * 64 : (h + 1) * 64, :, :],
+                out=w_view[:, w_cuts[h] // PACK : w_cuts[h + 1] // PACK, :, :],
                 in_=w_raw[h][:].rearrange("p j (m t) -> p m j t", t=PACK),
             )
 
-        def quantize(src, name):
-            codes = sb([P, S], U32, name + "_w")
-            scales = sb([P, S], U8, name + "_s")
-            nc.vector.quantize_mx(out=codes[:].bitcast(FP8X4), scales=scales[:], in_=src[:])
-            return codes, scales
-
-        w_w, w_s = quantize(w_bf, "wq")
-        xc_w = pick(x_w, cand_t, U32, "xc_w", 512)
+        w_w = sb([P, H], U32, "w_w")
+        w_s = sb([P, H], U8, "w_s")
+        for h in range(2):
+            cols = slice(h * H // 2, (h + 1) * H // 2)
+            nc.vector.quantize_mx(
+                out=w_w[:, cols].bitcast(FP8X4),
+                scales=w_s[:, cols],
+                in_=w_bf[:, PACK * cols.start : PACK * cols.stop],
+            )
         dk_g = pick(d_s, k1_t, U8, "dk_g", 0)
-        dk_w = pick(d_w, k1_t, U32, "dk_w", 2560)
         dk_s = sb([P, H], U8, "dk_s")
         nc.vector.tensor_copy(dk_s[:].bitcast(I32), dk_g[:].bitcast(I32))
         for e in range(2):
-            nc.gpsimd.dma_start(dk_s[2 + e : P : 32, :].bitcast(I32), dk_g[16 + e : P : 32, :].bitcast(I32))
+            nc.sync.dma_start(dk_s[2 + e : P : 32, :].bitcast(I32), dk_g[16 + e : P : 32, :].bitcast(I32))
+        xc_w = pick(x_w, cand_t, U32, "xc_w", 512)
+        dk_w = pick(d_w, k1_t, U32, "dk_w", 2560)
 
         def product(lhs_w, lhs_s, rhs_w, rhs_s, block, bank):
             acc = psum.tile([P, S], F32, name=f"acc{bank}", tag=f"bank{bank}")
@@ -130,7 +141,10 @@ def tile_picked_cdkeypullbhopdrms_none_p_kernel(
             sq_w = sb([P, WINDOW], F32, f"sq_win{t}")
             nc.scalar.activation(sq_w[:, :S], acc[:], ACT.Square)
             sq_p = sb([P, S], F32, f"sq_pl{t}")
-            nc.sync.dma_start(sq_p[:], sq_w[:, :S])
+            if t < 2:
+                nc.gpsimd.tensor_scalar(sq_p[:], sq_w[:, :S], 1.0, 0.0, ALU.mult, ALU.add)
+            else:
+                nc.sync.dma_start(sq_p[:], sq_w[:, :S])
             sq_win.append(sq_w)
             sq_pl.append(sq_p)
         for t in range(PACK):
@@ -140,6 +154,9 @@ def tile_picked_cdkeypullbhopdrms_none_p_kernel(
             nc.sync.dma_start(y_p[:], y_w[:, :S])
             y_win.append(y_w)
             y_pl.append(y_p)
+
+        gs16 = sb([P, PACK], F32, "gs16")
+        nc.gpsimd.tensor_scalar(gs16[:], gs_t[:], SCORE_SCALE, 0.0, ALU.mult, ALU.add)
 
         y4, st = [], []
         for t in range(PACK):
@@ -153,86 +170,114 @@ def tile_picked_cdkeypullbhopdrms_none_p_kernel(
             )
         rs = sb([P, PACK * S], F32, "rs")
         nc.scalar.activation(rs[:], den[:], ACT.Abs_reciprocal_sqrt, bias=quarter[:])
-        for t in range(PACK):
-            s = sb([P, WINDOW], F32, f"st{t}", f"sq_win{PACK - 1 - t}")
+
+        def step(t, s):
             nc.vector.tensor_tensor(s[:, :S], y_win[t][:].indirect(n1_t[:]), y_pl[t][:], ALU.subtract)
             st.append(s)
 
-        def interleave(planes, name):
-            woven = sb([P, S, PACK], BF16, name)
+        for t in range(PACK - 1):
+            step(t, sb([P, WINDOW], F32, f"st{t}", f"sq_win{PACK - 1 - t}"))
+
+        def interleave(planes, name, kib):
+            woven = placed([P, S, PACK], BF16, name, kib)
             nc.vector.tensor_copy(
                 out=woven[:].rearrange("p (c i) t -> p c t i", i=4),
                 in_=planes[:].rearrange("p t (c i) -> p c t i", i=4),
             )
             return woven
 
-        z2_pl = sb([P, PACK, S], BF16, "z2_pl")
+        z2_pl = placed([P, PACK, S], BF16, "z2_pl", 0)
         for t in range(PACK):
             nc.vector.scalar_tensor_tensor(
                 z2_pl[:, t, :], y4[t][:], gk_t[:, t : t + 1], rs[:, t * S : (t + 1) * S], ALU.mult, ALU.mult
             )
+        z2_bf = interleave(z2_pl, "z2_bf", 6)
+        step(PACK - 1, placed([P, WINDOW], F32, "st_last", 2))
         sig = sb([P, PACK * S], F32, "sig", "den")
         for t in range(PACK):
             nc.scalar.activation(sig[:, t * S : (t + 1) * S], st[t][:].indirect(n2_t[:]), ACT.Sigmoid)
-        z2_bf = interleave(z2_pl, "z2_bf")
-        z_pl = sb([P, PACK, S], BF16, "z_pl", "z2_pl")
-
-        def z_plane(t):
-            nc.vector.scalar_tensor_tensor(
-                z_pl[:, t, :], y_pl[t][:], gs_t[:, t : t + 1], sig[:, t * S : (t + 1) * S], ALU.mult, ALU.mult
-            )
-
-        z_plane(0)
         z2_w = sb([P, S], U32, "z2_w")
         z2_s = sb([P, S], U8, "z2_s")
         nc.vector.quantize_mx(
             out=z2_w[:].bitcast(FP8X4), scales=z2_s[:], in_=z2_bf[:].rearrange("p c t -> p (c t)")
         )
-        for t in range(1, PACK):
-            z_plane(t)
-        z_bf = interleave(z_pl, "z_bf")
+        z_pl = placed([P, PACK, S], BF16, "z_pl", 6)
+        for t in range(PACK):
+            nc.vector.scalar_tensor_tensor(
+                z_pl[:, t, :], y_pl[t][:], gs16[:, t : t + 1], sig[:, t * S : (t + 1) * S], ALU.mult, ALU.mult
+            )
+        z_bf = interleave(z_pl, "z_bf", 12)
+
+        b_acc, a_acc, b6, a_win, diff, gate, rest, pull = {}, {}, {}, {}, {}, {}, {}, {}
+
+        def keys(m, b_win):
+            nc.scalar.activation(b_win[:, :S], b_acc[m][:], ACT.Copy, scale=SCORE_SCALE)
+            b6[m] = sb([P, S], F32, f"b6_{m}")
+            nc.scalar.activation(b6[m][:], b_win[:].indirect(n6_t[:]), ACT.Copy)
+
+        def difference(m, tile):
+            diff[m] = tile
+            nc.vector.scalar_tensor_tensor(tile[:], b_acc[m][:], -SCORE_SCALE, b6[m][:], ALU.mult, ALU.add)
+
+        def sigmoid(m, tile):
+            gate[m] = tile
+            nc.scalar.activation(tile[:], diff[m][:], ACT.Sigmoid)
+
+        def window(m, tile, copy):
+            a_win[m] = tile
+            copy(out=tile[:, :S], in_=a_acc[m][:])
+
+        def terms(m):
+            rest[m] = sb([P, S], F32, f"rest{m}")
+            nc.vector.scalar_tensor_tensor(rest[m][:], gate[m][:], 1.0, a_acc[m][:], ALU.subtract, ALU.mult)
+            pull[m] = sb([P, S], F32, f"pull{m}")
+            nc.vector.tensor_tensor(pull[m][:], a_win[m][:].indirect(n5_t[:]), gate[m][:], ALU.mult)
+
+        def store(m):
+            res = sb([P, S], F32, f"res{m}")
+            nc.vector.tensor_tensor(res[:], pull[m][:], rest[m][:], ALU.subtract)
+            nc.sync.dma_start(out[m * P : (m + 1) * P, :], res[:])
+
+        for m in range(PACK):
+            b_acc[m] = product(dk_w, dk_s, z2_w, z2_s, m, m)
+        keys(0, sb([P, WINDOW], F32, "b_win0"))
+        keys(1, sb([P, WINDOW], F32, "b_win1"))
+        difference(0, placed([P, S], F32, "diff0", 8))
         z_w = sb([P, S], U32, "z_w")
         z_s = sb([P, S], U8, "z_s")
         nc.vector.quantize_mx(
             out=z_w[:].bitcast(FP8X4), scales=z_s[:], in_=z_bf[:].rearrange("p c t -> p (c t)")
         )
-
-        b_win, b6, a_win, gate = {}, {}, {}, {}
-
-        def keys(m, bank):
-            acc = product(dk_w, dk_s, z2_w, z2_s, m, bank)
-            b_win[m] = sb([P, WINDOW], F32, f"b_win{m}")
-            nc.scalar.activation(b_win[m][:, :S], acc[:], ACT.Copy, scale=SCORE_SCALE)
-            b6[m] = sb([P, S], F32, f"b6_{m}")
-            nc.scalar.activation(b6[m][:], b_win[m][:].indirect(n6_t[:]), ACT.Copy)
-
-        def candidates(m, bank):
-            acc = product(xc_w, xc_s, z_w, z_s, m, bank)
-            diff = sb([P, S], F32, f"diff{m}")
-            nc.vector.tensor_tensor(diff[:], b6[m][:], b_win[m][:, :S], ALU.subtract)
-            a_win[m] = sb([P, WINDOW], F32, f"a_win{m}")
-            nc.scalar.activation(a_win[m][:, :S], acc[:], ACT.Copy, scale=SCORE_SCALE)
-            gate[m] = sb([P, S], F32, f"gate{m}")
-            nc.scalar.activation(gate[m][:], diff[:], ACT.Sigmoid)
-
-        def blend(m):
-            rest = sb([P, S], F32, f"rest{m}")
-            nc.vector.scalar_tensor_tensor(rest[:], gate[m][:], 1.0, a_win[m][:, :S], ALU.subtract, ALU.mult)
-            pull = sb([P, S], F32, f"pull{m}")
-            nc.vector.tensor_tensor(pull[:], a_win[m][:].indirect(n5_t[:]), gate[m][:], ALU.mult)
-            res = sb([P, S], F32, f"res{m}")
-            nc.vector.tensor_tensor(res[:], pull[:], rest[:], ALU.subtract)
-            nc.sync.dma_start(out[m * P : (m + 1) * P, :], res[:])
-
-        keys(0, 4)
-        keys(1, 5)
-        candidates(0, 6)
-        candidates(1, 7)
-        keys(2, 6)
-        keys(3, 7)
-        blend(0)
-        blend(1)
-        candidates(2, 4)
-        candidates(3, 5)
-        blend(2)
-        blend(3)
+        for m in range(PACK):
+            a_acc[m] = product(xc_w, xc_s, z_w, z_s, m, PACK + m)
+        difference(1, placed([P, S], F32, "diff1", 14))
+        sigmoid(0, placed([P, S], F32, "gate0", 18))
+        window(0, sb([P, WINDOW], F32, "a_win0"), nc.vector.tensor_copy)
+        keys(2, placed([P, WINDOW], F32, "b_win2", 8))
+        terms(0)
+        sigmoid(1, sb([P, S], F32, "gate1"))
+        window(1, placed([P, WINDOW], F32, "a_win1", 8), nc.scalar.copy)
+        keys(3, placed([P, WINDOW], F32, "b_win3", 14))
+        difference(2, placed([P, S], F32, "diff2", 18))
+        store(0)
+        terms(1)
+        difference(3, sb([P, S], F32, "diff3", "gate1"))
+        store(1)
+        sigmoid(2, sb([P, S], F32, "gate2"))
+        window(2, placed([P, WINDOW], F32, "a_win2", 14), nc.scalar.copy)
+        window(3, placed([P, WINDOW], F32, "a_win3", 18), nc.scalar.copy)
+        a5 = sb([P, S], F32, "a5")
+        nc.scalar.activation(a5[:], a_win[3][:].indirect(n5_t[:]), ACT.Copy)
+        sigmoid(3, sb([P, S], F32, "gate3"))
+        terms(2)
+        away = sb([P, S], F32, "away")
+        nc.vector.tensor_tensor(away[:], a5[:], a_acc[3][:], ALU.subtract)
+        store(2)
+        move = sb([P, S], F32, "move")
+        res = sb([P, S], F32, "res_last")
+        halves = [slice(0, S // 2), slice(S // 2, S)]
+        for cols in halves:
+            nc.vector.tensor_tensor(move[:, cols], away[:, cols], gate[3][:, cols], ALU.mult)
+        for cols in halves:
+            nc.vector.tensor_tensor(res[:, cols], move[:, cols], a_acc[3][:, cols], ALU.add)
+            nc.sync.dma_start(out[3 * P : 4 * P, cols], res[:, cols])

@@ -113,10 +113,6 @@ def tile_picked_cdkeypullbhopdrms_none_p_kernel(
                 in_=w_bf[:, PACK * cols.start : PACK * cols.stop],
             )
         dk_g = pick(d_s, k1_t, U8, "dk_g", 0)
-        dk_s = sb([P, H], U8, "dk_s")
-        nc.vector.tensor_copy(dk_s[:].bitcast(I32), dk_g[:].bitcast(I32))
-        for e in range(2):
-            nc.sync.dma_start(dk_s[2 + e : P : 32, :].bitcast(I32), dk_g[16 + e : P : 32, :].bitcast(I32))
         xc_w = pick(x_w, cand_t, U32, "xc_w", 512)
         dk_w = pick(d_w, k1_t, U32, "dk_w", 2560)
 
@@ -141,8 +137,8 @@ def tile_picked_cdkeypullbhopdrms_none_p_kernel(
             sq_w = sb([P, WINDOW], F32, f"sq_win{t}")
             nc.scalar.activation(sq_w[:, :S], acc[:], ACT.Square)
             sq_p = sb([P, S], F32, f"sq_pl{t}")
-            if t < 2:
-                nc.gpsimd.tensor_scalar(sq_p[:], sq_w[:, :S], 1.0, 0.0, ALU.mult, ALU.add)
+            if t == 0:
+                nc.vector.tensor_copy(sq_p[:], sq_w[:, :S])
             else:
                 nc.sync.dma_start(sq_p[:], sq_w[:, :S])
             sq_win.append(sq_w)
@@ -155,9 +151,6 @@ def tile_picked_cdkeypullbhopdrms_none_p_kernel(
             y_win.append(y_w)
             y_pl.append(y_p)
 
-        gs16 = sb([P, PACK], F32, "gs16")
-        nc.gpsimd.tensor_scalar(gs16[:], gs_t[:], SCORE_SCALE, 0.0, ALU.mult, ALU.add)
-
         y4, st = [], []
         for t in range(PACK):
             g = sb([P, S], F32, f"y4_{t}")
@@ -168,6 +161,12 @@ def tile_picked_cdkeypullbhopdrms_none_p_kernel(
             nc.vector.tensor_tensor(
                 den[:, t * S : (t + 1) * S], sq_win[t][:].indirect(n3_t[:]), sq_pl[t][:], ALU.add
             )
+        gs16 = sb([P, PACK], F32, "gs16", "sq_pl0")
+        nc.vector.tensor_scalar_mul(gs16[:], gs_t[:], SCORE_SCALE)
+        dk_s = sb([P, H], U8, "dk_s", "sq_pl1")
+        nc.vector.tensor_copy(dk_s[:].bitcast(I32), dk_g[:].bitcast(I32))
+        for e in range(2):
+            nc.sync.dma_start(dk_s[2 + e : P : 32, :].bitcast(I32), dk_g[16 + e : P : 32, :].bitcast(I32))
         rs = sb([P, PACK * S], F32, "rs")
         nc.scalar.activation(rs[:], den[:], ACT.Abs_reciprocal_sqrt, bias=quarter[:])
 

@@ -47,6 +47,7 @@ def tile_picked_cdkeypullbhopdrms_none_p_kernel(
         x_s = sb([P, T], U8, "x_s")
         d_w = sb([P, G], U32, "d_w")
         d_s = sb([P, G], U8, "d_s")
+        nc.gpsimd.memset(x_s[:].bitcast(I32), 0)
         nc.gpsimd.memset(d_s[:].bitcast(I32), 0)
         quarter = sb([P, 1], F32, "quarter")
         sixteen = sb([P, 1], F32, "sixteen")
@@ -54,19 +55,17 @@ def tile_picked_cdkeypullbhopdrms_none_p_kernel(
         nc.scalar.activation(quarter[:], sixteen[:], ACT.Abs_reciprocal_sqrt)
 
         offs_t = load_list(offs, "offs_t")
-        for q in range(4):
-            rows = x_scales[0, 4 * q : 4 * q + 4, :].bitcast(I32)
-            nc.sync.dma_start(
-                x_s[32 * q : 32 * (q + 1), :].bitcast(I32), rows.unsqueeze(0).to_broadcast([8, 4, T // 4])
-            )
         cand_t = load_list(cand, "cand_t")
+        for q in range(4):
+            nc.sync.dma_start(
+                x_s[32 * q : 32 * q + 4, :].bitcast(I32), x_scales[0, 4 * q : 4 * q + 4, :].bitcast(I32)
+            )
         w_rows = w1.rearrange("(p j) c -> p j c", j=PACK)
-        w_cuts = [0, H // 2, 3 * H // 4, H]
-        w_raw = [sb([P, PACK, w_cuts[h + 1] - w_cuts[h]], F32, f"w_raw{h}") for h in range(3)]
+        w_cuts = [0, 3 * H // 4, H]
+        w_raw = [sb([P, PACK, w_cuts[h + 1] - w_cuts[h]], F32, f"w_raw{h}") for h in range(2)]
         nc.sync.dma_start(w_raw[0][:], w_rows[:, :, : w_cuts[1]])
         nc.sync.dma_start(x_w[:].bitcast(I32), x_words[0].rearrange("p n t -> p (n t)").bitcast(I32))
-        for h in (1, 2):
-            nc.sync.dma_start(w_raw[h][:], w_rows[:, :, w_cuts[h] : w_cuts[h + 1]])
+        nc.sync.dma_start(w_raw[1][:], w_rows[:, :, w_cuts[1] :])
         k1_t = load_list(k1, "k1_t")
         ds_rows = d_scales[0].rearrange("(r e) c -> e r c", e=2)
         for e in range(2):
@@ -97,7 +96,7 @@ def tile_picked_cdkeypullbhopdrms_none_p_kernel(
 
         w_bf = head.tile([P, PACK * H], BF16, name="w_bf", align_bytes=64, offset=0)
         w_view = w_bf[:].rearrange("p (t m j) -> p m j t", t=PACK, j=PACK)
-        for h in range(3):
+        for h in range(2):
             nc.scalar.copy(
                 out=w_view[:, w_cuts[h] // PACK : w_cuts[h + 1] // PACK, :, :],
                 in_=w_raw[h][:].rearrange("p j (m t) -> p m j t", t=PACK),

from contextlib import ExitStack

import concourse.mybir as mybir

K, T, S, H, C, G = 512, 1024, 512, 512, 512, 2048
FLOPS = 2 * K * H * S + 2 * K * C * S + 2 * K * H * S

F32 = mybir.dt.float32
BF16 = mybir.dt.bfloat16
I32 = mybir.dt.int32
U32 = mybir.dt.uint32
U16 = mybir.dt.uint16
U8 = mybir.dt.uint8
FP8X4 = mybir.dt.float8_e4m3fn_x4
ACT = mybir.ActivationFunctionType
ALU = mybir.AluOpType

P = 128
PACK = 4
WINDOW = 2 * S
SCORE_SCALE = 0.0625


def tile_picked_cdkeypullbhopdrms_none_p_kernel(
    tc, x_words, x_scales, w1, gs, gk, d_words, d_scales, offs, n1, n2, n3, n4, cand, k1, n5, n6, out
):
    nc = tc.nc
    with ExitStack() as ctx:
        lists = ctx.enter_context(tc.tile_pool(name="lists", bufs=1))
        keep = ctx.enter_context(tc.tile_pool(name="keep", bufs=1))
        head = ctx.enter_context(tc.tile_pool(name="head", bufs=1))
        mid = ctx.enter_context(tc.tile_pool(name="mid", bufs=1))
        psum = ctx.enter_context(tc.psum_pool(name="psum", bufs=1))

        def placed(shape, dtype, name, kib):
            return mid.tile(shape, dtype, name=name, align_bytes=64, offset=kib * 1024)

        def load_list(src, name):
            tile = lists.tile([P, S // 16], U16, name=name)
            nc.sync.dma_start(tile[:], src)
            return tile

        def sb(shape, dtype, name, tag=None):
            return keep.tile(shape, dtype, name=name, tag=tag or name, align_bytes=64)

        x_w = sb([P, T], U32, "x_w")
        x_s = sb([P, T], U8, "x_s")
        d_w = sb([P, G], U32, "d_w")
        d_s = sb([P, G], U8, "d_s")
        nc.gpsimd.memset(x_s[:].bitcast(I32), 0)
        nc.gpsimd.memset(d_s[:].bitcast(I32), 0)
        quarter = sb([P, 1], F32, "quarter")
        sixteen = sb([P, 1], F32, "sixteen")
        nc.vector.memset(sixteen[:], 16.0)
        nc.scalar.activation(quarter[:], sixteen[:], ACT.Abs_reciprocal_sqrt)

        offs_t = load_list(offs, "offs_t")
        cand_t = load_list(cand, "cand_t")
        for q in range(4):
            nc.sync.dma_start(
                x_s[32 * q : 32 * q + 4, :].bitcast(I32), x_scales[0, 4 * q : 4 * q + 4, :].bitcast(I32)
            )
        w_rows = w1.rearrange("(p j) c -> p j c", j=PACK)
        w_cuts = [0, 3 * H // 4, H]
        w_raw = [sb([P, PACK, w_cuts[h + 1] - w_cuts[h]], F32, f"w_raw{h}") for h in range(2)]
        nc.sync.dma_start(w_raw[0][:], w_rows[:, :, : w_cuts[1]])
        nc.sync.dma_start(x_w[:].bitcast(I32), x_words[0].rearrange("p n t -> p (n t)").bitcast(I32))
        nc.sync.dma_start(w_raw[1][:], w_rows[:, :, w_cuts[1] :])
        k1_t = load_list(k1, "k1_t")
        ds_rows = d_scales[0].rearrange("(r e) c -> e r c", e=2)
        for e in range(2):
            nc.sync.dma_start(d_s[e:P:16, :].bitcast(I32), ds_rows[e].bitcast(I32))
        nc.sync.dma_start(d_w[:].bitcast(I32), d_words[0].rearrange("p n t -> p (n t)").bitcast(I32))
        n3_t = load_list(n3, "n3_t")
        n4_t = load_list(n4, "n4_t")
        n1_t = load_list(n1, "n1_t")
        n2_t = load_list(n2, "n2_t")
        gs_t = sb([P, PACK], F32, "gs_t")
        gk_t = sb([P, PACK], F32, "gk_t")
        nc.sync.dma_start(gk_t[:], gk.rearrange("(p t) o -> p (t o)", t=PACK))
        nc.sync.dma_start(gs_t[:], gs.rearrange("(p t) o -> p (t o)", t=PACK))
        n6_t = load_list(n6, "n6_t")
        n5_t = load_list(n5, "n5_t")

        def pick(table, offsets, dtype, name, offset=None):
            if offset is None:
                picked = sb([P, S], dtype, name)
            else:
                picked = head.tile([P, S], dtype, name=name, align_bytes=64, offset=offset)
            nc.vector.tensor_copy(picked[:], table[:].indirect(offsets[:]))
            return picked

        xq_s = pick(x_s, offs_t, U8, "xq_s")
        xc_s = pick(x_s, cand_t, U8, "xc_s")
        xq_w = pick(x_w, offs_t, U32, "xq_w")

        w_bf = head.tile([P, PACK * H], BF16, name="w_bf", align_bytes=64, offset=0)
        w_view = w_bf[:].rearrange("p (t m j) -> p m j t", t=PACK, j=PACK)
        for h in range(2):
            nc.scalar.copy(
                out=w_view[:, w_cuts[h] // PACK : w_cuts[h + 1] // PACK, :, :],
                in_=w_raw[h][:].rearrange("p j (m t) -> p m j t", t=PACK),
            )

        w_w = sb([P, H], U32, "w_w")
        w_s = sb([P, H], U8, "w_s")
        for h in range(2):
            cols = slice(h * H // 2, (h + 1) * H // 2)
            nc.vector.quantize_mx(
                out=w_w[:, cols].bitcast(FP8X4),
                scales=w_s[:, cols],
                in_=w_bf[:, PACK * cols.start : PACK * cols.stop],
            )
        dk_g = pick(d_s, k1_t, U8, "dk_g", 0)
        xc_w = pick(x_w, cand_t, U32, "xc_w", 512)
        dk_w = pick(d_w, k1_t, U32, "dk_w", 2560)

        def product(lhs_w, lhs_s, rhs_w, rhs_s, block, bank):
            acc = psum.tile([P, S], F32, name=f"acc{bank}", tag=f"bank{bank}")
            cols = slice(block * P, (block + 1) * P)
            nc.tensor.matmul_mx(
                out=acc[:],
                lhsT=lhs_w[:, cols].bitcast(FP8X4),
                lhsT_scale=lhs_s[:, cols],
                rhs=rhs_w[:].bitcast(FP8X4),
                rhs_scale=rhs_s[:],
                start=True,
                stop=True,
            )
            return acc

        y_win, y_pl, sq_win, sq_pl = [], [], [], []
        y_acc = [product(w_w, w_s, xq_w, xq_s, t, t) for t in range(PACK)]
        for t in range(PACK):
            acc = y_acc[t]
            sq_w = sb([P, WINDOW], F32, f"sq_win{t}")
            nc.scalar.activation(sq_w[:, :S], acc[:], ACT.Square)
            sq_p = sb([P, S], F32, f"sq_pl{t}")
            if t == 0:
                nc.vector.tensor_copy(sq_p[:], sq_w[:, :S])
            else:
                nc.sync.dma_start(sq_p[:], sq_w[:, :S])
            sq_win.append(sq_w)
            sq_pl.append(sq_p)
        for t in range(PACK):
            y_w = sb([P, WINDOW], F32, f"y_win{t}")
            nc.scalar.copy(out=y_w[:, :S], in_=y_acc[t][:])
            y_p = sb([P, S], F32, f"y_pl{t}")
            nc.sync.dma_start(y_p[:], y_w[:, :S])
            y_win.append(y_w)
            y_pl.append(y_p)

        y4, st = [], []
        for t in range(PACK):
            g = sb([P, S], F32, f"y4_{t}")
            nc.scalar.activation(g[:], y_win[t][:].indirect(n4_t[:]), ACT.Copy)
            y4.append(g)
        den = sb([P, PACK * S], F32, "den", "den")
        for t in range(PACK):
            nc.vector.tensor_tensor(
                den[:, t * S : (t + 1) * S], sq_win[t][:].indirect(n3_t[:]), sq_pl[t][:], ALU.add
            )
        gs16 = sb([P, PACK], F32, "gs16", "sq_pl0")
        nc.vector.tensor_scalar_mul(gs16[:], gs_t[:], SCORE_SCALE)
        dk_s = sb([P, H], U8, "dk_s", "sq_pl1")
        nc.vector.tensor_copy(dk_s[:].bitcast(I32), dk_g[:].bitcast(I32))
        for e in range(2):
            nc.sync.dma_start(dk_s[2 + e : P : 32, :].bitcast(I32), dk_g[16 + e : P : 32, :].bitcast(I32))
        rs = sb([P, PACK * S], F32, "rs")
        nc.scalar.activation(rs[:], den[:], ACT.Abs_reciprocal_sqrt, bias=quarter[:])

        def step(t, s):
            nc.vector.tensor_tensor(s[:, :S], y_win[t][:].indirect(n1_t[:]), y_pl[t][:], ALU.subtract)
            st.append(s)

        for t in range(PACK - 1):
            step(t, sb([P, WINDOW], F32, f"st{t}", f"sq_win{PACK - 1 - t}"))

        def interleave(planes, name, kib):
            woven = placed([P, S, PACK], BF16, name, kib)
            nc.vector.tensor_copy(
                out=woven[:].rearrange("p (c i) t -> p c t i", i=4),
                in_=planes[:].rearrange("p t (c i) -> p c t i", i=4),
            )
            return woven

        z2_pl = placed([P, PACK, S], BF16, "z2_pl", 0)
        for t in range(PACK):
            nc.vector.scalar_tensor_tensor(
                z2_pl[:, t, :], y4[t][:], gk_t[:, t : t + 1], rs[:, t * S : (t + 1) * S], ALU.mult, ALU.mult
            )
        z2_bf = interleave(z2_pl, "z2_bf", 6)
        step(PACK - 1, placed([P, WINDOW], F32, "st_last", 2))
        sig = sb([P, PACK * S], F32, "sig", "den")
        for t in range(PACK):
            nc.scalar.activation(sig[:, t * S : (t + 1) * S], st[t][:].indirect(n2_t[:]), ACT.Sigmoid)
        z2_w = sb([P, S], U32, "z2_w")
        z2_s = sb([P, S], U8, "z2_s")
        nc.vector.quantize_mx(
            out=z2_w[:].bitcast(FP8X4), scales=z2_s[:], in_=z2_bf[:].rearrange("p c t -> p (c t)")
        )
        z_pl = placed([P, PACK, S], BF16, "z_pl", 6)
        for t in range(PACK):
            nc.vector.scalar_tensor_tensor(
                z_pl[:, t, :], y_pl[t][:], gs16[:, t : t + 1], sig[:, t * S : (t + 1) * S], ALU.mult, ALU.mult
            )
        z_bf = interleave(z_pl, "z_bf", 12)

        b_acc, a_acc, b6, a_win, diff, gate, rest, pull = {}, {}, {}, {}, {}, {}, {}, {}

        def keys(m, b_win):
            nc.scalar.activation(b_win[:, :S], b_acc[m][:], ACT.Copy, scale=SCORE_SCALE)
            b6[m] = sb([P, S], F32, f"b6_{m}")
            nc.scalar.activation(b6[m][:], b_win[:].indirect(n6_t[:]), ACT.Copy)

        def difference(m, tile):
            diff[m] = tile
            nc.vector.scalar_tensor_tensor(tile[:], b_acc[m][:], -SCORE_SCALE, b6[m][:], ALU.mult, ALU.add)

        def sigmoid(m, tile):
            gate[m] = tile
            nc.scalar.activation(tile[:], diff[m][:], ACT.Sigmoid)

        def window(m, tile, copy):
            a_win[m] = tile
            copy(out=tile[:, :S], in_=a_acc[m][:])

        def terms(m):
            rest[m] = sb([P, S], F32, f"rest{m}")
            nc.vector.scalar_tensor_tensor(rest[m][:], gate[m][:], 1.0, a_acc[m][:], ALU.subtract, ALU.mult)
            pull[m] = sb([P, S], F32, f"pull{m}")
            nc.vector.tensor_tensor(pull[m][:], a_win[m][:].indirect(n5_t[:]), gate[m][:], ALU.mult)

        def store(m):
            res = sb([P, S], F32, f"res{m}")
            nc.vector.tensor_tensor(res[:], pull[m][:], rest[m][:], ALU.subtract)
            nc.sync.dma_start(out[m * P : (m + 1) * P, :], res[:])

        for m in range(PACK):
            b_acc[m] = product(dk_w, dk_s, z2_w, z2_s, m, m)
        keys(0, sb([P, WINDOW], F32, "b_win0"))
        keys(1, sb([P, WINDOW], F32, "b_win1"))
        difference(0, placed([P, S], F32, "diff0", 8))
        z_w = sb([P, S], U32, "z_w")
        z_s = sb([P, S], U8, "z_s")
        nc.vector.quantize_mx(
            out=z_w[:].bitcast(FP8X4), scales=z_s[:], in_=z_bf[:].rearrange("p c t -> p (c t)")
        )
        for m in range(PACK):
            a_acc[m] = product(xc_w, xc_s, z_w, z_s, m, PACK + m)
        difference(1, placed([P, S], F32, "diff1", 14))
        sigmoid(0, placed([P, S], F32, "gate0", 18))
        window(0, sb([P, WINDOW], F32, "a_win0"), nc.vector.tensor_copy)
        keys(2, placed([P, WINDOW], F32, "b_win2", 8))
        terms(0)
        sigmoid(1, sb([P, S], F32, "gate1"))
        window(1, placed([P, WINDOW], F32, "a_win1", 8), nc.scalar.copy)
        keys(3, placed([P, WINDOW], F32, "b_win3", 14))
        difference(2, placed([P, S], F32, "diff2", 18))
        store(0)
        terms(1)
        difference(3, sb([P, S], F32, "diff3", "gate1"))
        store(1)
        sigmoid(2, sb([P, S], F32, "gate2"))
        window(2, placed([P, WINDOW], F32, "a_win2", 14), nc.scalar.copy)
        window(3, placed([P, WINDOW], F32, "a_win3", 18), nc.scalar.copy)
        a5 = sb([P, S], F32, "a5")
        nc.scalar.activation(a5[:], a_win[3][:].indirect(n5_t[:]), ACT.Copy)
        sigmoid(3, sb([P, S], F32, "gate3"))
        terms(2)
        away = sb([P, S], F32, "away")
        nc.vector.tensor_tensor(away[:], a5[:], a_acc[3][:], ALU.subtract)
        store(2)
        move = sb([P, S], F32, "move")
        res = sb([P, S], F32, "res_last")
        halves = [slice(0, S // 2), slice(S // 2, S)]
        for cols in halves:
            nc.vector.tensor_tensor(move[:, cols], away[:, cols], gate[3][:, cols], ALU.mult)
        for cols in halves:
            nc.vector.tensor_tensor(res[:, cols], move[:, cols], a_acc[3][:, cols], ALU.add)
            nc.sync.dma_start(out[3 * P : 4 * P, cols], res[:, cols])
